import numpy as np
import ml_dtypes


def mxq(x, axis, fmt="e4m3"):
    dtype, down = {"e4m3": (ml_dtypes.float8_e4m3fn, 7), "e5m2": (ml_dtypes.float8_e5m2, 14)}[fmt]
    v = np.moveaxis(np.asarray(x, np.float32).astype(ml_dtypes.bfloat16).astype(np.float64), axis, -1)
    blocks = v.reshape(v.shape[:-1] + (-1, 32))
    amax = np.abs(blocks).max(-1, keepdims=True)
    byte = np.maximum(np.where(amax > 0, np.frexp(amax)[1] - 1 + 127, 0) - down, 1)
    scale = np.exp2(byte - 127.0)
    codes = (blocks / scale).astype(np.float32).astype(dtype).astype(np.float64)
    return np.moveaxis((codes * scale).reshape(v.shape), -1, axis)


WIDE = False


def mx_kscale(k):
    if not WIDE:
        return np.ones(k)
    levels = np.array([10, -10, 5, -5, 0])
    if k % 512:
        return np.exp2(np.random.permutation(np.resize(levels, k // 32))).repeat(32)
    a = np.empty((k // 512, 16))
    for p in range(k // 512):
        a[p, :8] = np.random.permutation(np.resize(levels, 8))
        for g in range(8):
            far = levels[np.abs(levels - a[p, g]) >= 10]
            a[p, g + 8] = far[np.random.randint(len(far))]
    return np.exp2(a.ravel()).repeat(32)


def f64(x):
    return np.asarray(x).astype(np.float64)


def striped(idx):
    return np.tile(np.asarray(idx).reshape(-1, 16).T, (8, 1)).astype(np.uint16)


def unstriped(offs):
    return offs[:16].T.reshape(-1).astype(np.int64)


E2M1 = np.array([0.0, 0.5, 1.0, 1.5, 2.0, 3.0, 4.0, 6.0, -0.0, -0.5, -1.0, -1.5, -2.0, -3.0, -4.0, -6.0])


def pack_weight(w, fmt):
    k, n = w.shape
    w = f64(np.asarray(w, np.float32).astype(ml_dtypes.bfloat16)).reshape(k // 32, 32, n)
    amax = np.abs(w).max(1)
    if fmt == "e4m3":
        byte = np.frexp(amax)[1] - 1 + 127 - 7
    else:
        mant, ex = np.frexp(amax / 6.0)
        byte = np.where(mant > 0.5, ex, ex - 1) + 127
    byte = np.clip(np.where(amax > 0, byte, 1), 1, 254)
    scaled = (w * np.exp2(127.0 - byte)[:, None, :]).reshape(k, n).astype(np.float32)
    by_word = np.ascontiguousarray(scaled.reshape(k // 512, 128, 4, n).transpose(0, 1, 3, 2))
    if fmt == "e4m3":
        words = by_word.astype(ml_dtypes.float8_e4m3fn).view(np.uint8)
    else:
        c = by_word.astype(ml_dtypes.float4_e2m1fn).view(np.uint8) & 0xF
        words = (c[..., 0::2] | (c[..., 1::2] << 4)).reshape(k // 512, 128, 2 * n)
    return np.ascontiguousarray(words), np.ascontiguousarray(byte.astype(np.uint8).reshape(k // 512, 16, n))


def unpack_weight(words, scales, fmt):
    g, _, n = scales.shape
    words = np.ascontiguousarray(words).reshape(g, 128, n, -1)
    if fmt == "e4m3":
        vals = words.view(ml_dtypes.float8_e4m3fn).astype(np.float64)
    else:
        nib = np.empty((g, 128, n, 4), np.uint8)
        nib[..., 0::2] = words & 0xF
        nib[..., 1::2] = words >> 4
        vals = E2M1[nib]
    vals = vals * np.repeat(np.exp2(scales.astype(np.float64) - 127.0), 8, axis=1)[..., None]
    return vals.transpose(0, 1, 3, 2).reshape(g * 512, n)


def sigmoid(v):
    return 1.0 / (1.0 + np.exp(-v))


D, E, T, I, Q, G, U = 512, 512, 2048, 512, 128, 64, 256


def setup_inputs():
    n = np.random.standard_normal
    idx2 = np.random.permutation(U)[:G]
    idx = np.random.permutation(T)[:I]
    fd = mx_kscale(D)
    fe = mx_kscale(E)
    keysp = pack_weight(n((D, T)) / fd[:, None], "e4m3")
    valsp = pack_weight(n((E, T)) / fe[:, None], "e4m3")
    return {
        "query": (n((D, Q)) * 0.7 / np.sqrt(D) * fd[:, None]).astype(np.float32),
        "pquery": (n((D, Q)) * 1.0 / np.sqrt(D) * fd[:, None]).astype(np.float32),
        "keys_words": keysp[0],
        "keys_scales": keysp[1],
        "pgsum": (n((D, U)) / fd[:, None]).astype(np.float32),
        "reserve": (np.random.uniform(20.0, 100.0, (Q, 1))).astype(np.float32),
        "gout": (n((E, Q)) * 1 / np.sqrt(E) * fe[:, None]).astype(np.float32),
        "vals_words": valsp[0],
        "vals_scales": valsp[1],
        "dquery": (n((D, Q)) * 1.0 / np.sqrt(D) * fd[:, None]).astype(np.float32),
        "base": (0.5 * n((Q, T))).astype(np.float32),
        "offs2": striped(idx2),
        "offs": striped(idx),
    }


def reference(query, pquery, keys_words, keys_scales, pgsum, reserve, gout, vals_words, vals_scales, dquery, base, offs2, offs):
    idx2 = unstriped(offs2)
    idx = unstriped(offs)
    keysu = unpack_weight(keys_words, keys_scales, "e4m3")
    valsu = unpack_weight(vals_words, vals_scales, "e4m3")
    pqueryq = mxq(f64(pquery), 0, "e4m3")
    pgsumidx2q = mxq(f64(pgsum)[:, idx2], 0, "e4m3")
    h0 = pqueryq.T @ pgsumidx2q
    g1 = sigmoid(h0)
    gr = np.repeat(g1, I // G, axis=1)
    queryq = mxq(f64(query), 0, "e4m3")
    keysidxg = keysu[:, idx]
    a = queryq.T @ keysidxg
    dqueryq = mxq(f64(dquery), 0, "e4m3")
    ta = dqueryq.T @ keysidxg
    p = np.exp(a) * gr
    z = np.sum(p, axis=1, keepdims=True) + f64(reserve)
    goutq = mxq(f64(gout), 0, "e4m3")
    valsidxg = valsu[:, idx]
    c0 = goutq.T @ valsidxg
    dz = np.sum(c0 * p / np.square(z) * (-1.0), axis=1, keepdims=True)
    dp = c0 / z + dz
    tp = ta * np.exp(a) * gr
    tz = np.sum(tp, axis=1, keepdims=True)
    tdz = np.sum((tp * c0 - tz * z * 2.0 * c0 * p / np.square(z)) / np.square(z) * (-1.0), axis=1, keepdims=True)
    tdp = tz * c0 / np.square(z) * (-1.0) + tdz
    tda = tdp * gr * np.exp(a) + ta * np.exp(a) * dp * gr
    gs = tda * 512.0
    gf = np.zeros((Q, T))
    gf[:, idx] = gs
    y = f64(base) + gf
    return y

@@ -1,0 +1,179 @@
+from contextlib import ExitStack
+
+import concourse.mybir as mybir
+
+D, T, I, Q, G, U = 512, 2048, 512, 128, 64, 256
+FLOPS = 2 * D * Q * (3 * I + G)
+
+F32 = mybir.dt.float32
+BF16 = mybir.dt.bfloat16
+I32 = mybir.dt.int32
+U32 = mybir.dt.uint32
+U16 = mybir.dt.uint16
+U8 = mybir.dt.uint8
+FP8X4 = mybir.dt.float8_e4m3fn_x4
+ALU = mybir.AluOpType
+ACT = mybir.ActivationFunctionType
+
+P = 128
+PACK = 4
+PAGE = I // G
+GS_SCALE = 512.0
+OUT_CHUNKS = (512, 512, 512, 512)
+
+
+def tile_attend_hvpagetablegate_s_kernel(tc, query, pquery, keys_words, keys_scales, pgsum, reserve, gout,
+                                          vals_words, vals_scales, dquery, base, offs2, offs, out):
+    nc = tc.nc
+    with ExitStack() as ctx:
+        sb = ctx.enter_context(tc.tile_pool(name="sb", bufs=1))
+        ps = ctx.enter_context(tc.psum_pool(name="ps", bufs=1))
+
+        def tile(name, shape, dtype):
+            return sb.tile(shape, dtype, name=name, align_bytes=64)
+
+        tok_list = tile("tok_list", [P, I // 16], U16)
+        page_list = tile("page_list", [P, G // 16], U16)
+        k_words = tile("k_words", [P, T], U32)
+        v_words = tile("v_words", [P, T], U32)
+        k_bytes = tile("k_bytes", [P, T], U8)
+        v_bytes = tile("v_bytes", [P, T], U8)
+        window = tile("window", [P, T], F32)
+        base_sb = tile("base_sb", [P, T], F32)
+        pg_raw = tile("pg_raw", [P, PACK, U], F32)
+        reserve_sb = tile("reserve_sb", [P, 1], F32)
+        warm = tile("warm", [P, 1], F32)
+        warm_out = tile("warm_out", [P, 1], F32)
+
+        nc.vector.memset(k_bytes[:, :T // 2].bitcast(I32), 0)
+        nc.gpsimd.memset(k_bytes[:, T // 2:].bitcast(I32), 0)
+        nc.gpsimd.memset(v_bytes[:].bitcast(I32), 0)
+        nc.gpsimd.memset(window[:], 0.0)
+        nc.vector.memset(warm[:], 0.0)
+        nc.scalar.activation(warm_out[:], warm[:], ACT.Sigmoid)
+
+        def load_bytes(dst, src, row0, quads):
+            for quad in quads:
+                lo = 32 * quad + row0
+                nc.sync.dma_start(dst[lo:lo + 4, :].bitcast(I32), src[0, 4 * quad:4 * quad + 4, :].bitcast(I32))
+
+        def load_words(dst, src):
+            nc.sync.dma_start(dst[:].bitcast(I32), src[0].rearrange("p n t -> p (n t)").bitcast(I32))
+
+        raw = {}
+
+        def load_rows(name, src):
+            raw[name] = tile(name + "_raw", [P, PACK, Q], F32)
+            nc.sync.dma_start(raw[name][:], src.rearrange("(p j) w -> p j w", j=PACK))
+
+        nc.sync.dma_start(page_list[:], offs2)
+        nc.sync.dma_start(tok_list[:], offs)
+        nc.sync.dma_start(reserve_sb[:], reserve)
+        nc.sync.dma_start(pg_raw[:], pgsum.rearrange("(p j) w -> p j w", j=PACK))
+        load_rows("pq", pquery)
+        load_bytes(k_bytes, keys_scales, 0, range(4))
+        load_words(k_words, keys_words)
+        load_rows("q", query)
+        load_bytes(v_bytes, vals_scales, 4, range(4))
+        load_rows("dq", dquery)
+        load_words(v_words, vals_words)
+        load_rows("go", gout)
+        nc.sync.dma_start(base_sb[:], base)
+
+        def quantize(name, grouped, width):
+            codes = tile(name + "_codes", [P, width], U32)
+            scales = tile(name + "_scales", [P, width], U8)
+            nc.vector.quantize_mx(out=codes[:].bitcast(FP8X4), scales=scales[:],
+                                  in_=grouped[:].rearrange("p w j -> p (w j)"))
+            return codes, scales
+
+        def interleave(name):
+            grouped = tile(name + "_bf", [P, Q, PACK], BF16)
+            nc.scalar.copy(grouped[:], raw[name][:].rearrange("p j w -> p w j"))
+            return grouped
+
+        def product(name, rows, codes, scales_ap, width):
+            acc = ps.tile([P, width], F32, name=name)
+            nc.tensor.matmul_mx(out=acc[:], lhsT=rows[0][:].bitcast(FP8X4), lhsT_scale=rows[1][:],
+                                rhs=codes[:].bitcast(FP8X4), rhs_scale=scales_ap, start=True, stop=True)
+            return acc
+
+        def gather(name, pool_tile, dtype):
+            picked = tile(name, [P, I], dtype)
+            nc.vector.tensor_copy(picked[:], pool_tile[:].indirect(tok_list[:]))
+            return picked
+
+        pg_bf = tile("pg_bf", [P, G, PACK], BF16)
+        for j in range(PACK):
+            nc.vector.tensor_copy(pg_bf[:, :, j], pg_raw[:, j, :].indirect(page_list[:]))
+        pq_bf = interleave("pq")
+        pg_mx = quantize("pg", pg_bf, G)
+        kb = gather("kb", k_bytes, U8)
+        pq_mx = quantize("pq", pq_bf, Q)
+        h0 = product("h0", pq_mx, pg_mx[0], pg_mx[1][:], G)
+        gate = tile("gate", [P, G, 1], F32)
+        nc.scalar.activation(gate[:].rearrange("p g o -> p (g o)"), h0[:], ACT.Sigmoid)
+        warm_exp = tile("warm_exp", [P, 1], F32)
+        nc.scalar.activation(warm_exp[:], gate[:, 0, :], ACT.Exp)
+
+        q_bf = interleave("q")
+        dq_bf = interleave("dq")
+        kw = gather("kw", k_words, U32)
+        q_mx = quantize("q", q_bf, Q)
+        a = product("a", q_mx, kw, kb[:], I)
+        vb = gather("vb", v_bytes, U8)
+        dq_mx = quantize("dq", dq_bf, Q)
+        ta = product("ta", dq_mx, kw, kb[:], I)
+
+        neg_a = tile("neg_a", [P, I], F32)
+        neg_m = tile("neg_m", [P, 1], F32)
+        nc.vector.tensor_scalar(neg_a[:], a[:], -1.0, 0.0, ALU.mult, ALU.min, accum_out=neg_m[:])
+        e = tile("e", [P, I], F32)
+        nc.scalar.activation(e[:], neg_a[:], ACT.Exp, bias=neg_m[:], scale=-1.0)
+        shrink = tile("shrink", [P, 1], F32)
+        nc.scalar.activation(shrink[:], neg_m[:], ACT.Exp)
+        res_s = tile("res_s", [P, 1], F32)
+        nc.scalar.activation(res_s[:], shrink[:], ACT.Copy, scale=reserve_sb[:])
+        go_bf = interleave("go")
+
+        vw = gather("vw", v_words, U32)
+        go_mx = quantize("go", go_bf, Q)
+        c0 = product("c0", go_mx, vw, vb[4:P, :], I)
+
+        p = tile("p", [P, I], F32)
+        z0 = tile("z0", [P, 1], F32)
+        nc.vector.scalar_tensor_tensor(p[:].rearrange("p (g j) -> p g j", j=PAGE),
+                                       e[:].rearrange("p (g j) -> p g j", j=PAGE), 1.0,
+                                       gate[:].to_broadcast([P, G, PAGE]), ALU.mult, ALU.mult, accum_out=z0[:])
+        z_s = tile("z_s", [P, 1], F32)
+        nc.vector.tensor_scalar(z_s[:], z0[:], res_s[:], 1.0 / GS_SCALE, ALU.add, ALU.mult)
+        big_r = tile("big_r", [P, 1], F32)
+        nc.vector.reciprocal(big_r[:], z_s[:])
+        neg_r = tile("neg_r", [P, 1], F32)
+        nc.scalar.mul(neg_r[:], big_r[:], -1.0 / GS_SCALE)
+        pn = tile("pn", [P, I], F32)
+        nc.scalar.activation(pn[:], p[:], ACT.Copy, scale=neg_r[:])
+        wt = tile("wt", [P, I], F32)
+        wt_sum = tile("wt_sum", [P, 1], F32)
+        nc.vector.scalar_tensor_tensor(wt[:], ta[:], big_r[:], p[:], ALU.mult, ALU.mult, accum_out=wt_sum[:])
+        u = tile("u", [P, I], F32)
+        nc.vector.scalar_tensor_tensor(u[:], pn[:], wt_sum[:], wt[:], ALU.mult, ALU.add)
+        y = tile("y", [P, I], F32)
+        y_sum = tile("y_sum", [P, 1], F32)
+        nc.vector.scalar_tensor_tensor(y[:], c0[:], 1.0, u[:], ALU.mult, ALU.mult, accum_out=y_sum[:])
+        pc = tile("pc", [P, I], F32)
+        neg_s = tile("neg_s", [P, 1], F32)
+        nc.vector.scalar_tensor_tensor(pc[:], c0[:], 1.0, pn[:], ALU.mult, ALU.mult, accum_out=neg_s[:])
+        kp = tile("kp", [P, I], F32)
+        nc.scalar.activation(kp[:], pn[:], ACT.Copy, scale=y_sum[:])
+        rest = tile("rest", [P, I], F32)
+        nc.vector.scalar_tensor_tensor(rest[:], u[:], neg_s[:], y[:], ALU.mult, ALU.add)
+        nc.vector.tensor_tensor(window[:].indirect(tok_list[:]), rest[:], kp[:], ALU.add)
+
+        lo = 0
+        for n, width in enumerate(OUT_CHUNKS):
+            cols = slice(lo, lo + width)
+            res = tile("res%d" % n, [P, width], F32)
+            nc.vector.tensor_tensor(res[:], window[:, cols], base_sb[:, cols], ALU.add)
+            nc.sync.dma_start(out[:, cols], res[:])
+            lo += width

@@ -45,8 +45,7 @@ def tile_attend_hvpagetablegate_s_kernel(tc, query, pquery, keys_words, keys_sca
         warm = tile("warm", [P, 1], F32)
         warm_out = tile("warm_out", [P, 1], F32)
 
-        nc.vector.memset(k_bytes[:, :T // 2].bitcast(I32), 0)
-        nc.gpsimd.memset(k_bytes[:, T // 2:].bitcast(I32), 0)
+        nc.gpsimd.memset(k_bytes[:].bitcast(I32), 0)
         nc.gpsimd.memset(v_bytes[:].bitcast(I32), 0)
         nc.gpsimd.memset(window[:], 0.0)
         nc.vector.memset(warm[:], 0.0)
@@ -71,9 +70,9 @@ def tile_attend_hvpagetablegate_s_kernel(tc, query, pquery, keys_words, keys_sca
         nc.sync.dma_start(reserve_sb[:], reserve)
         nc.sync.dma_start(pg_raw[:], pgsum.rearrange("(p j) w -> p j w", j=PACK))
         load_rows("pq", pquery)
+        load_rows("q", query)
         load_bytes(k_bytes, keys_scales, 0, range(4))
         load_words(k_words, keys_words)
-        load_rows("q", query)
         load_bytes(v_bytes, vals_scales, 4, range(4))
         load_rows("dq", dquery)
         load_words(v_words, vals_words)
@@ -106,7 +105,10 @@ def tile_attend_hvpagetablegate_s_kernel(tc, query, pquery, keys_words, keys_sca
         pg_bf = tile("pg_bf", [P, G, PACK], BF16)
         for j in range(PACK):
             nc.vector.tensor_copy(pg_bf[:, :, j], pg_raw[:, j, :].indirect(page_list[:]))
+        res_512 = tile("res_512", [P, 1], F32)
+        nc.scalar.mul(res_512[:], reserve_sb[:], 1.0 / GS_SCALE)
         pq_bf = interleave("pq")
+        q_bf = interleave("q")
         pg_mx = quantize("pg", pg_bf, G)
         kb = gather("kb", k_bytes, U8)
         pq_mx = quantize("pq", pq_bf, Q)
@@ -116,7 +118,6 @@ def tile_attend_hvpagetablegate_s_kernel(tc, query, pquery, keys_words, keys_sca
         warm_exp = tile("warm_exp", [P, 1], F32)
         nc.scalar.activation(warm_exp[:], gate[:, 0, :], ACT.Exp)
 
-        q_bf = interleave("q")
         dq_bf = interleave("dq")
         kw = gather("kw", k_words, U32)
         q_mx = quantize("q", q_bf, Q)
@@ -125,50 +126,57 @@ def tile_attend_hvpagetablegate_s_kernel(tc, query, pquery, keys_words, keys_sca
         dq_mx = quantize("dq", dq_bf, Q)
         ta = product("ta", dq_mx, kw, kb[:], I)
 
-        neg_a = tile("neg_a", [P, I], F32)
+        neg_a = sb.tile([P, I], F32, name="neg_a", tag="v_bytes", align_bytes=64)
         neg_m = tile("neg_m", [P, 1], F32)
         nc.vector.tensor_scalar(neg_a[:], a[:], -1.0, 0.0, ALU.mult, ALU.min, accum_out=neg_m[:])
-        e = tile("e", [P, I], F32)
+        e = sb.tile([P, I], F32, name="e", tag="dq_raw", align_bytes=64)
         nc.scalar.activation(e[:], neg_a[:], ACT.Exp, bias=neg_m[:], scale=-1.0)
         shrink = tile("shrink", [P, 1], F32)
         nc.scalar.activation(shrink[:], neg_m[:], ACT.Exp)
         res_s = tile("res_s", [P, 1], F32)
-        nc.scalar.activation(res_s[:], shrink[:], ACT.Copy, scale=reserve_sb[:])
+        nc.scalar.activation(res_s[:], shrink[:], ACT.Copy, scale=res_512[:])
         go_bf = interleave("go")
 
         vw = gather("vw", v_words, U32)
         go_mx = quantize("go", go_bf, Q)
         c0 = product("c0", go_mx, vw, vb[4:P, :], I)
 
-        p = tile("p", [P, I], F32)
-        z0 = tile("z0", [P, 1], F32)
+        def column(name):
+            return tile(name, [P, 1], F32)
+
+        p = sb.tile([P, I], F32, name="p", tag="v_words", align_bytes=64)
+        z0 = column("z0")
         nc.vector.scalar_tensor_tensor(p[:].rearrange("p (g j) -> p g j", j=PAGE),
                                        e[:].rearrange("p (g j) -> p g j", j=PAGE), 1.0,
                                        gate[:].to_broadcast([P, G, PAGE]), ALU.mult, ALU.mult, accum_out=z0[:])
-        z_s = tile("z_s", [P, 1], F32)
-        nc.vector.tensor_scalar(z_s[:], z0[:], res_s[:], 1.0 / GS_SCALE, ALU.add, ALU.mult)
-        big_r = tile("big_r", [P, 1], F32)
+        z_s = column("z_s")
+        nc.scalar.activation(z_s[:], z0[:], ACT.Identity, bias=res_s[:], scale=1.0 / GS_SCALE)
+        pt = sb.tile([P, I], F32, name="pt", tag="go_bf", align_bytes=64)
+        tz = column("tz")
+        nc.vector.scalar_tensor_tensor(pt[:], ta[:], 1.0, p[:], ALU.mult, ALU.mult, accum_out=tz[:])
+        big_r = column("big_r")
         nc.vector.reciprocal(big_r[:], z_s[:])
-        neg_r = tile("neg_r", [P, 1], F32)
+        neg_r = column("neg_r")
         nc.scalar.mul(neg_r[:], big_r[:], -1.0 / GS_SCALE)
+        neg_t = column("neg_t")
+        nc.scalar.activation(neg_t[:], tz[:], ACT.Copy, scale=neg_r[:])
         pn = tile("pn", [P, I], F32)
         nc.scalar.activation(pn[:], p[:], ACT.Copy, scale=neg_r[:])
-        wt = tile("wt", [P, I], F32)
-        wt_sum = tile("wt_sum", [P, 1], F32)
-        nc.vector.scalar_tensor_tensor(wt[:], ta[:], big_r[:], p[:], ALU.mult, ALU.mult, accum_out=wt_sum[:])
-        u = tile("u", [P, I], F32)
-        nc.vector.scalar_tensor_tensor(u[:], pn[:], wt_sum[:], wt[:], ALU.mult, ALU.add)
-        y = tile("y", [P, I], F32)
-        y_sum = tile("y_sum", [P, 1], F32)
-        nc.vector.scalar_tensor_tensor(y[:], c0[:], 1.0, u[:], ALU.mult, ALU.mult, accum_out=y_sum[:])
         pc = tile("pc", [P, I], F32)
-        neg_s = tile("neg_s", [P, 1], F32)
-        nc.vector.scalar_tensor_tensor(pc[:], c0[:], 1.0, pn[:], ALU.mult, ALU.mult, accum_out=neg_s[:])
-        kp = tile("kp", [P, I], F32)
-        nc.scalar.activation(kp[:], pn[:], ACT.Copy, scale=y_sum[:])
+        s_big = column("s_big")
+        nc.vector.scalar_tensor_tensor(pc[:], c0[:], big_r[:], p[:], ALU.mult, ALU.mult, accum_out=s_big[:])
+        u = tile("u", [P, I], F32)
+        nc.vector.scalar_tensor_tensor(u[:], ta[:], neg_t[:], p[:], ALU.add, ALU.mult)
+        neg_sr = column("neg_sr")
+        nc.scalar.activation(neg_sr[:], s_big[:], ACT.Copy, scale=neg_r[:])
+        us = tile("us", [P, I], F32)
+        nc.scalar.activation(us[:], u[:], ACT.Copy, scale=neg_sr[:])
+        y = tile("y", [P, I], F32)
+        y_sum = column("y_sum")
+        nc.vector.scalar_tensor_tensor(y[:], c0[:], big_r[:], u[:], ALU.mult, ALU.mult, accum_out=y_sum[:])
         rest = tile("rest", [P, I], F32)
-        nc.vector.scalar_tensor_tensor(rest[:], u[:], neg_s[:], y[:], ALU.mult, ALU.add)
-        nc.vector.tensor_tensor(window[:].indirect(tok_list[:]), rest[:], kp[:], ALU.add)
+        nc.vector.scalar_tensor_tensor(rest[:], pn[:], y_sum[:], y[:], ALU.mult, ALU.add)
+        nc.vector.tensor_tensor(window[:].indirect(tok_list[:]), rest[:], us[:], ALU.add)
 
         lo = 0
         for n, width in enumerate(OUT_CHUNKS):

@@ -67,14 +67,14 @@ def tile_attend_hvpagetablegate_s_kernel(tc, query, pquery, keys_words, keys_sca
 
         nc.sync.dma_start(page_list[:], offs2)
         nc.sync.dma_start(tok_list[:], offs)
-        nc.sync.dma_start(reserve_sb[:], reserve)
         nc.sync.dma_start(pg_raw[:], pgsum.rearrange("(p j) w -> p j w", j=PACK))
         load_rows("pq", pquery)
         load_rows("q", query)
         load_bytes(k_bytes, keys_scales, 0, range(4))
         load_words(k_words, keys_words)
-        load_bytes(v_bytes, vals_scales, 4, range(4))
         load_rows("dq", dquery)
+        load_bytes(v_bytes, vals_scales, 4, range(4))
+        nc.sync.dma_start(reserve_sb[:], reserve)
         load_words(v_words, vals_words)
         load_rows("go", gout)
         nc.sync.dma_start(base_sb[:], base)
@@ -97,16 +97,14 @@ def tile_attend_hvpagetablegate_s_kernel(tc, query, pquery, keys_words, keys_sca
                                 rhs=codes[:].bitcast(FP8X4), rhs_scale=scales_ap, start=True, stop=True)
             return acc
 
-        def gather(name, pool_tile, dtype):
-            picked = tile(name, [P, I], dtype)
+        def gather(name, pool_tile, dtype, tag=None):
+            picked = sb.tile([P, I], dtype, name=name, tag=tag or name, align_bytes=64)
             nc.vector.tensor_copy(picked[:], pool_tile[:].indirect(tok_list[:]))
             return picked
 
         pg_bf = tile("pg_bf", [P, G, PACK], BF16)
         for j in range(PACK):
             nc.vector.tensor_copy(pg_bf[:, :, j], pg_raw[:, j, :].indirect(page_list[:]))
-        res_512 = tile("res_512", [P, 1], F32)
-        nc.scalar.mul(res_512[:], reserve_sb[:], 1.0 / GS_SCALE)
         pq_bf = interleave("pq")
         q_bf = interleave("q")
         pg_mx = quantize("pg", pg_bf, G)
@@ -122,27 +120,31 @@ def tile_attend_hvpagetablegate_s_kernel(tc, query, pquery, keys_words, keys_sca
         kw = gather("kw", k_words, U32)
         q_mx = quantize("q", q_bf, Q)
         a = product("a", q_mx, kw, kb[:], I)
-        vb = gather("vb", v_bytes, U8)
         dq_mx = quantize("dq", dq_bf, Q)
+        vb = gather("vb", v_bytes, U8, tag="dq_bf")
         ta = product("ta", dq_mx, kw, kb[:], I)
 
-        neg_a = sb.tile([P, I], F32, name="neg_a", tag="v_bytes", align_bytes=64)
-        neg_m = tile("neg_m", [P, 1], F32)
-        nc.vector.tensor_scalar(neg_a[:], a[:], -1.0, 0.0, ALU.mult, ALU.min, accum_out=neg_m[:])
-        e = sb.tile([P, I], F32, name="e", tag="dq_raw", align_bytes=64)
-        nc.scalar.activation(e[:], neg_a[:], ACT.Exp, bias=neg_m[:], scale=-1.0)
-        shrink = tile("shrink", [P, 1], F32)
+        def column(name):
+            return tile(name, [P, 1], F32)
+
+        a_bf = sb.tile([P, I], BF16, name="a_bf", tag="dq_raw", align_bytes=64)
+        nc.scalar.copy(a_bf[:], a[:])
+        neg_a = sb.tile([P, I], BF16, name="neg_a", tag="v_bytes", align_bytes=64)
+        neg_m = column("neg_m")
+        nc.vector.tensor_scalar(neg_a[:], a_bf[:], -1.0, 0.0, ALU.mult, ALU.min, accum_out=neg_m[:])
+        e = tile("e", [P, I], F32)
+        nc.scalar.activation(e[:], a[:], ACT.Exp, bias=neg_m[:])
+        shrink = column("shrink")
         nc.scalar.activation(shrink[:], neg_m[:], ACT.Exp)
-        res_s = tile("res_s", [P, 1], F32)
-        nc.scalar.activation(res_s[:], shrink[:], ACT.Copy, scale=res_512[:])
         go_bf = interleave("go")
+        res_512 = column("res_512")
+        nc.scalar.mul(res_512[:], reserve_sb[:], 1.0 / GS_SCALE)
+        res_s = column("res_s")
+        nc.scalar.activation(res_s[:], shrink[:], ACT.Copy, scale=res_512[:])
 
         vw = gather("vw", v_words, U32)
         go_mx = quantize("go", go_bf, Q)
         c0 = product("c0", go_mx, vw, vb[4:P, :], I)
-
-        def column(name):
-            return tile(name, [P, 1], F32)
 
         p = sb.tile([P, I], F32, name="p", tag="v_words", align_bytes=64)
         z0 = column("z0")
@@ -151,13 +153,13 @@ def tile_attend_hvpagetablegate_s_kernel(tc, query, pquery, keys_words, keys_sca
                                        gate[:].to_broadcast([P, G, PAGE]), ALU.mult, ALU.mult, accum_out=z0[:])
         z_s = column("z_s")
         nc.scalar.activation(z_s[:], z0[:], ACT.Identity, bias=res_s[:], scale=1.0 / GS_SCALE)
-        pt = sb.tile([P, I], F32, name="pt", tag="go_bf", align_bytes=64)
-        tz = column("tz")
-        nc.vector.scalar_tensor_tensor(pt[:], ta[:], 1.0, p[:], ALU.mult, ALU.mult, accum_out=tz[:])
-        big_r = column("big_r")
+        big_r = sb.tile([P, 1], F32, name="big_r", tag="go_bf", align_bytes=64)
         nc.vector.reciprocal(big_r[:], z_s[:])
         neg_r = column("neg_r")
         nc.scalar.mul(neg_r[:], big_r[:], -1.0 / GS_SCALE)
+        pt = sb.tile([P, I], F32, name="pt", tag="z_s", align_bytes=64)
+        tz = column("tz")
+        nc.vector.scalar_tensor_tensor(pt[:], ta[:], 1.0, p[:], ALU.mult, ALU.mult, accum_out=tz[:])
         neg_t = column("neg_t")
         nc.scalar.activation(neg_t[:], tz[:], ACT.Copy, scale=neg_r[:])
         pn = tile("pn", [P, I], F32)
@@ -165,18 +167,18 @@ def tile_attend_hvpagetablegate_s_kernel(tc, query, pquery, keys_words, keys_sca
         pc = tile("pc", [P, I], F32)
         s_big = column("s_big")
         nc.vector.scalar_tensor_tensor(pc[:], c0[:], big_r[:], p[:], ALU.mult, ALU.mult, accum_out=s_big[:])
-        u = tile("u", [P, I], F32)
-        nc.vector.scalar_tensor_tensor(u[:], ta[:], neg_t[:], p[:], ALU.add, ALU.mult)
-        neg_sr = column("neg_sr")
-        nc.scalar.activation(neg_sr[:], s_big[:], ACT.Copy, scale=neg_r[:])
-        us = tile("us", [P, I], F32)
-        nc.scalar.activation(us[:], u[:], ACT.Copy, scale=neg_sr[:])
+        pts = tile("pts", [P, I], F32)
+        s_r = column("s_r")
+        nc.scalar.activation(s_r[:], s_big[:], ACT.Copy, scale=neg_r[:])
+        nc.scalar.activation(pts[:], pt[:], ACT.Copy, scale=s_r[:])
         y = tile("y", [P, I], F32)
         y_sum = column("y_sum")
-        nc.vector.scalar_tensor_tensor(y[:], c0[:], big_r[:], u[:], ALU.mult, ALU.mult, accum_out=y_sum[:])
+        nc.vector.scalar_tensor_tensor(y[:], ta[:], neg_t[:], pc[:], ALU.add, ALU.mult, accum_out=y_sum[:])
+        beta = column("beta")
+        nc.vector.tensor_scalar(beta[:], s_big[:], neg_t[:], y_sum[:], ALU.mult, ALU.add)
         rest = tile("rest", [P, I], F32)
-        nc.vector.scalar_tensor_tensor(rest[:], pn[:], y_sum[:], y[:], ALU.mult, ALU.add)
-        nc.vector.tensor_tensor(window[:].indirect(tok_list[:]), rest[:], us[:], ALU.add)
+        nc.vector.scalar_tensor_tensor(rest[:], pn[:], beta[:], y[:], ALU.mult, ALU.add)
+        nc.vector.tensor_tensor(window[:].indirect(tok_list[:]), rest[:], pts[:], ALU.add)
 
         lo = 0
         for n, width in enumerate(OUT_CHUNKS):

@@ -51,8 +51,8 @@ def tile_attend_hvpagetablegate_s_kernel(tc, query, pquery, keys_words, keys_sca
         nc.vector.memset(warm[:], 0.0)
         nc.scalar.activation(warm_out[:], warm[:], ACT.Sigmoid)
 
-        def load_bytes(dst, src, row0, quads):
-            for quad in quads:
+        def load_bytes(dst, src, row0):
+            for quad in (0, 2, 1, 3):
                 lo = 32 * quad + row0
                 nc.sync.dma_start(dst[lo:lo + 4, :].bitcast(I32), src[0, 4 * quad:4 * quad + 4, :].bitcast(I32))
 
@@ -67,14 +67,14 @@ def tile_attend_hvpagetablegate_s_kernel(tc, query, pquery, keys_words, keys_sca
 
         nc.sync.dma_start(page_list[:], offs2)
         nc.sync.dma_start(tok_list[:], offs)
+        nc.sync.dma_start(reserve_sb[:], reserve)
         nc.sync.dma_start(pg_raw[:], pgsum.rearrange("(p j) w -> p j w", j=PACK))
         load_rows("pq", pquery)
         load_rows("q", query)
-        load_bytes(k_bytes, keys_scales, 0, range(4))
+        load_bytes(k_bytes, keys_scales, 0)
         load_words(k_words, keys_words)
+        load_bytes(v_bytes, vals_scales, 4)
         load_rows("dq", dquery)
-        load_bytes(v_bytes, vals_scales, 4, range(4))
-        nc.sync.dma_start(reserve_sb[:], reserve)
         load_words(v_words, vals_words)
         load_rows("go", gout)
         nc.sync.dma_start(base_sb[:], base)
@@ -97,14 +97,16 @@ def tile_attend_hvpagetablegate_s_kernel(tc, query, pquery, keys_words, keys_sca
                                 rhs=codes[:].bitcast(FP8X4), rhs_scale=scales_ap, start=True, stop=True)
             return acc
 
-        def gather(name, pool_tile, dtype, tag=None):
-            picked = sb.tile([P, I], dtype, name=name, tag=tag or name, align_bytes=64)
+        def gather(name, pool_tile, dtype):
+            picked = tile(name, [P, I], dtype)
             nc.vector.tensor_copy(picked[:], pool_tile[:].indirect(tok_list[:]))
             return picked
 
         pg_bf = tile("pg_bf", [P, G, PACK], BF16)
         for j in range(PACK):
             nc.vector.tensor_copy(pg_bf[:, :, j], pg_raw[:, j, :].indirect(page_list[:]))
+        res_512 = tile("res_512", [P, 1], F32)
+        nc.scalar.mul(res_512[:], reserve_sb[:], 1.0 / GS_SCALE)
         pq_bf = interleave("pq")
         q_bf = interleave("q")
         pg_mx = quantize("pg", pg_bf, G)
@@ -120,27 +122,23 @@ def tile_attend_hvpagetablegate_s_kernel(tc, query, pquery, keys_words, keys_sca
         kw = gather("kw", k_words, U32)
         q_mx = quantize("q", q_bf, Q)
         a = product("a", q_mx, kw, kb[:], I)
+        vb = gather("vb", v_bytes, U8)
         dq_mx = quantize("dq", dq_bf, Q)
-        vb = gather("vb", v_bytes, U8, tag="dq_bf")
         ta = product("ta", dq_mx, kw, kb[:], I)
 
         def column(name):
             return tile(name, [P, 1], F32)
 
-        a_bf = sb.tile([P, I], BF16, name="a_bf", tag="dq_raw", align_bytes=64)
-        nc.scalar.copy(a_bf[:], a[:])
-        neg_a = sb.tile([P, I], BF16, name="neg_a", tag="v_bytes", align_bytes=64)
+        neg_a = sb.tile([P, I], F32, name="neg_a", tag="v_bytes", align_bytes=64)
         neg_m = column("neg_m")
-        nc.vector.tensor_scalar(neg_a[:], a_bf[:], -1.0, 0.0, ALU.mult, ALU.min, accum_out=neg_m[:])
-        e = tile("e", [P, I], F32)
-        nc.scalar.activation(e[:], a[:], ACT.Exp, bias=neg_m[:])
+        nc.vector.tensor_scalar(neg_a[:], a[:], -1.0, 0.0, ALU.mult, ALU.min, accum_out=neg_m[:])
+        e = sb.tile([P, I], F32, name="e", tag="dq_raw", align_bytes=64)
+        nc.scalar.activation(e[:], neg_a[:], ACT.Exp, bias=neg_m[:], scale=-1.0)
         shrink = column("shrink")
         nc.scalar.activation(shrink[:], neg_m[:], ACT.Exp)
-        go_bf = interleave("go")
-        res_512 = column("res_512")
-        nc.scalar.mul(res_512[:], reserve_sb[:], 1.0 / GS_SCALE)
         res_s = column("res_s")
         nc.scalar.activation(res_s[:], shrink[:], ACT.Copy, scale=res_512[:])
+        go_bf = interleave("go")
 
         vw = gather("vw", v_words, U32)
         go_mx = quantize("go", go_bf, Q)

@@ -17,9 +17,13 @@ ACT = mybir.ActivationFunctionType
 
 P = 128
 PACK = 4
+QUADRANT = 32
+SCALE_ROWS = 4
+LIST_GROUP = 16
 PAGE = I // G
 GS_SCALE = 512.0
-OUT_CHUNKS = (512, 512, 512, 512)
+V_SCALE_ROW0 = 4
+OUT_CHUNK = 512
 
 
 def tile_attend_hvpagetablegate_s_kernel(tc, query, pquery, keys_words, keys_scales, pgsum, reserve, gout,
@@ -29,159 +33,155 @@ def tile_attend_hvpagetablegate_s_kernel(tc, query, pquery, keys_words, keys_sca
         sb = ctx.enter_context(tc.tile_pool(name="sb", bufs=1))
         ps = ctx.enter_context(tc.psum_pool(name="ps", bufs=1))
 
-        def tile(name, shape, dtype):
-            return sb.tile(shape, dtype, name=name, align_bytes=64)
+        def tile(name, shape, dtype, reuse=None):
+            return sb.tile(shape, dtype, name=name, tag=reuse or name, align_bytes=64)
 
-        tok_list = tile("tok_list", [P, I // 16], U16)
-        page_list = tile("page_list", [P, G // 16], U16)
+        def column(name, reuse=None):
+            return tile(name, [P, 1], F32, reuse)
+
+        tok_list = tile("tok_list", [P, I // LIST_GROUP], U16)
+        page_list = tile("page_list", [P, G // LIST_GROUP], U16)
         k_words = tile("k_words", [P, T], U32)
         v_words = tile("v_words", [P, T], U32)
         k_bytes = tile("k_bytes", [P, T], U8)
         v_bytes = tile("v_bytes", [P, T], U8)
-        window = tile("window", [P, T], F32)
+        gf = tile("gf", [P, T], F32)
         base_sb = tile("base_sb", [P, T], F32)
         pg_raw = tile("pg_raw", [P, PACK, U], F32)
-        reserve_sb = tile("reserve_sb", [P, 1], F32)
-        warm = tile("warm", [P, 1], F32)
-        warm_out = tile("warm_out", [P, 1], F32)
+        reserve_sb = column("reserve_sb")
 
         nc.gpsimd.memset(k_bytes[:].bitcast(I32), 0)
         nc.gpsimd.memset(v_bytes[:].bitcast(I32), 0)
-        nc.gpsimd.memset(window[:], 0.0)
-        nc.vector.memset(warm[:], 0.0)
-        nc.scalar.activation(warm_out[:], warm[:], ACT.Sigmoid)
+        nc.gpsimd.memset(gf[:], 0.0)
 
-        def load_bytes(dst, src, row0):
-            for quad in (0, 2, 1, 3):
-                lo = 32 * quad + row0
-                nc.sync.dma_start(dst[lo:lo + 4, :].bitcast(I32), src[0, 4 * quad:4 * quad + 4, :].bitcast(I32))
+        def load_scale_bytes(dst, src, row0):
+            for quad in range(P // QUADRANT):
+                lo = QUADRANT * quad + row0
+                rows = src[0, SCALE_ROWS * quad:SCALE_ROWS * (quad + 1), :]
+                nc.sync.dma_start(dst[lo:lo + SCALE_ROWS, :].bitcast(I32), rows.bitcast(I32))
 
         def load_words(dst, src):
             nc.sync.dma_start(dst[:].bitcast(I32), src[0].rearrange("p n t -> p (n t)").bitcast(I32))
 
-        raw = {}
-
         def load_rows(name, src):
-            raw[name] = tile(name + "_raw", [P, PACK, Q], F32)
-            nc.sync.dma_start(raw[name][:], src.rearrange("(p j) w -> p j w", j=PACK))
+            raw = tile(name, [P, PACK, Q], F32)
+            nc.sync.dma_start(raw[:], src.rearrange("(p t) w -> p t w", t=PACK))
+            return raw
 
         nc.sync.dma_start(page_list[:], offs2)
         nc.sync.dma_start(tok_list[:], offs)
         nc.sync.dma_start(reserve_sb[:], reserve)
-        nc.sync.dma_start(pg_raw[:], pgsum.rearrange("(p j) w -> p j w", j=PACK))
-        load_rows("pq", pquery)
-        load_rows("q", query)
-        load_bytes(k_bytes, keys_scales, 0)
+        nc.sync.dma_start(pg_raw[:], pgsum.rearrange("(p t) w -> p t w", t=PACK))
+        pq_raw = load_rows("pq_raw", pquery)
+        q_raw = load_rows("q_raw", query)
+        load_scale_bytes(k_bytes, keys_scales, 0)
         load_words(k_words, keys_words)
-        load_bytes(v_bytes, vals_scales, 4)
-        load_rows("dq", dquery)
+        load_scale_bytes(v_bytes, vals_scales, V_SCALE_ROW0)
+        dq_raw = load_rows("dq_raw", dquery)
         load_words(v_words, vals_words)
-        load_rows("go", gout)
+        go_raw = load_rows("go_raw", gout)
         nc.sync.dma_start(base_sb[:], base)
+
+        def interleave(name, raw):
+            grouped = tile(name, [P, Q, PACK], BF16)
+            nc.scalar.copy(grouped[:], raw[:].rearrange("p t w -> p w t"))
+            return grouped
 
         def quantize(name, grouped, width):
             codes = tile(name + "_codes", [P, width], U32)
             scales = tile(name + "_scales", [P, width], U8)
             nc.vector.quantize_mx(out=codes[:].bitcast(FP8X4), scales=scales[:],
-                                  in_=grouped[:].rearrange("p w j -> p (w j)"))
-            return codes, scales
-
-        def interleave(name):
-            grouped = tile(name + "_bf", [P, Q, PACK], BF16)
-            nc.scalar.copy(grouped[:], raw[name][:].rearrange("p j w -> p w j"))
-            return grouped
-
-        def product(name, rows, codes, scales_ap, width):
-            acc = ps.tile([P, width], F32, name=name)
-            nc.tensor.matmul_mx(out=acc[:], lhsT=rows[0][:].bitcast(FP8X4), lhsT_scale=rows[1][:],
-                                rhs=codes[:].bitcast(FP8X4), rhs_scale=scales_ap, start=True, stop=True)
-            return acc
+                                  in_=grouped[:].rearrange("p w t -> p (w t)"))
+            return codes, scales[:]
 
         def gather(name, pool_tile, dtype):
             picked = tile(name, [P, I], dtype)
             nc.vector.tensor_copy(picked[:], pool_tile[:].indirect(tok_list[:]))
             return picked
 
+        def product(name, rows, columns, width):
+            acc = ps.tile([P, width], F32, name=name)
+            nc.tensor.matmul_mx(out=acc[:], lhsT=rows[0][:].bitcast(FP8X4), lhsT_scale=rows[1],
+                                rhs=columns[0][:].bitcast(FP8X4), rhs_scale=columns[1], start=True, stop=True)
+            return acc
+
         pg_bf = tile("pg_bf", [P, G, PACK], BF16)
-        for j in range(PACK):
-            nc.vector.tensor_copy(pg_bf[:, :, j], pg_raw[:, j, :].indirect(page_list[:]))
-        res_512 = tile("res_512", [P, 1], F32)
-        nc.scalar.mul(res_512[:], reserve_sb[:], 1.0 / GS_SCALE)
-        pq_bf = interleave("pq")
-        q_bf = interleave("q")
+        for t in range(PACK):
+            nc.vector.tensor_copy(pg_bf[:, :, t], pg_raw[:, t, :].indirect(page_list[:]))
+        reserve_512 = column("reserve_512")
+        nc.scalar.mul(reserve_512[:], reserve_sb[:], 1.0 / GS_SCALE)
+        pq_bf = interleave("pq_bf", pq_raw)
+        q_bf = interleave("q_bf", q_raw)
         pg_mx = quantize("pg", pg_bf, G)
-        kb = gather("kb", k_bytes, U8)
+        k_bytes_listed = gather("k_bytes_listed", k_bytes, U8)
         pq_mx = quantize("pq", pq_bf, Q)
-        h0 = product("h0", pq_mx, pg_mx[0], pg_mx[1][:], G)
+        h0 = product("h0", pq_mx, pg_mx, G)
         gate = tile("gate", [P, G, 1], F32)
         nc.scalar.activation(gate[:].rearrange("p g o -> p (g o)"), h0[:], ACT.Sigmoid)
-        warm_exp = tile("warm_exp", [P, 1], F32)
-        nc.scalar.activation(warm_exp[:], gate[:, 0, :], ACT.Exp)
 
-        dq_bf = interleave("dq")
-        kw = gather("kw", k_words, U32)
+        dq_bf = interleave("dq_bf", dq_raw)
+        k_words_listed = gather("k_words_listed", k_words, U32)
+        keys_mx = (k_words_listed, k_bytes_listed[:])
         q_mx = quantize("q", q_bf, Q)
-        a = product("a", q_mx, kw, kb[:], I)
-        vb = gather("vb", v_bytes, U8)
+        a = product("a", q_mx, keys_mx, I)
+        v_bytes_listed = gather("v_bytes_listed", v_bytes, U8)
         dq_mx = quantize("dq", dq_bf, Q)
-        ta = product("ta", dq_mx, kw, kb[:], I)
+        ta = product("ta", dq_mx, keys_mx, I)
 
-        def column(name):
-            return tile(name, [P, 1], F32)
-
-        neg_a = sb.tile([P, I], F32, name="neg_a", tag="v_bytes", align_bytes=64)
+        neg_a = tile("neg_a", [P, I], F32, reuse="v_bytes")
         neg_m = column("neg_m")
         nc.vector.tensor_scalar(neg_a[:], a[:], -1.0, 0.0, ALU.mult, ALU.min, accum_out=neg_m[:])
-        e = sb.tile([P, I], F32, name="e", tag="dq_raw", align_bytes=64)
-        nc.scalar.activation(e[:], neg_a[:], ACT.Exp, bias=neg_m[:], scale=-1.0)
-        shrink = column("shrink")
-        nc.scalar.activation(shrink[:], neg_m[:], ACT.Exp)
-        res_s = column("res_s")
-        nc.scalar.activation(res_s[:], shrink[:], ACT.Copy, scale=res_512[:])
-        go_bf = interleave("go")
+        exp_a = tile("exp_a", [P, I], F32, reuse="dq_raw")
+        nc.scalar.activation(exp_a[:], neg_a[:], ACT.Exp, bias=neg_m[:], scale=-1.0)
+        exp_neg_m = column("exp_neg_m")
+        nc.scalar.activation(exp_neg_m[:], neg_m[:], ACT.Exp)
+        reserve_shifted = column("reserve_shifted")
+        nc.scalar.activation(reserve_shifted[:], exp_neg_m[:], ACT.Copy, scale=reserve_512[:])
+        go_bf = interleave("go_bf", go_raw)
 
-        vw = gather("vw", v_words, U32)
+        v_words_listed = gather("v_words_listed", v_words, U32)
         go_mx = quantize("go", go_bf, Q)
-        c0 = product("c0", go_mx, vw, vb[4:P, :], I)
+        c0 = product("c0", go_mx, (v_words_listed, v_bytes_listed[V_SCALE_ROW0:P, :]), I)
 
-        p = sb.tile([P, I], F32, name="p", tag="v_words", align_bytes=64)
-        z0 = column("z0")
+        p = tile("p", [P, I], F32, reuse="v_words")
+        p_sum = column("p_sum")
         nc.vector.scalar_tensor_tensor(p[:].rearrange("p (g j) -> p g j", j=PAGE),
-                                       e[:].rearrange("p (g j) -> p g j", j=PAGE), 1.0,
-                                       gate[:].to_broadcast([P, G, PAGE]), ALU.mult, ALU.mult, accum_out=z0[:])
-        z_s = column("z_s")
-        nc.scalar.activation(z_s[:], z0[:], ACT.Identity, bias=res_s[:], scale=1.0 / GS_SCALE)
-        big_r = sb.tile([P, 1], F32, name="big_r", tag="go_bf", align_bytes=64)
-        nc.vector.reciprocal(big_r[:], z_s[:])
+                                       exp_a[:].rearrange("p (g j) -> p g j", j=PAGE), 1.0,
+                                       gate[:].to_broadcast([P, G, PAGE]), ALU.mult, ALU.mult, accum_out=p_sum[:])
+        z_512 = column("z_512")
+        nc.scalar.activation(z_512[:], p_sum[:], ACT.Identity, bias=reserve_shifted[:], scale=1.0 / GS_SCALE)
+        r_512 = column("r_512", reuse="go_bf")
+        nc.vector.reciprocal(r_512[:], z_512[:])
         neg_r = column("neg_r")
-        nc.scalar.mul(neg_r[:], big_r[:], -1.0 / GS_SCALE)
-        pt = sb.tile([P, I], F32, name="pt", tag="z_s", align_bytes=64)
+        nc.scalar.mul(neg_r[:], r_512[:], -1.0 / GS_SCALE)
+
+        p_ta = tile("p_ta", [P, I], F32, reuse="z_512")
         tz = column("tz")
-        nc.vector.scalar_tensor_tensor(pt[:], ta[:], 1.0, p[:], ALU.mult, ALU.mult, accum_out=tz[:])
+        nc.vector.scalar_tensor_tensor(p_ta[:], ta[:], 1.0, p[:], ALU.mult, ALU.mult, accum_out=tz[:])
         neg_t = column("neg_t")
         nc.scalar.activation(neg_t[:], tz[:], ACT.Copy, scale=neg_r[:])
-        pn = tile("pn", [P, I], F32)
-        nc.scalar.activation(pn[:], p[:], ACT.Copy, scale=neg_r[:])
-        pc = tile("pc", [P, I], F32)
-        s_big = column("s_big")
-        nc.vector.scalar_tensor_tensor(pc[:], c0[:], big_r[:], p[:], ALU.mult, ALU.mult, accum_out=s_big[:])
-        pts = tile("pts", [P, I], F32)
-        s_r = column("s_r")
-        nc.scalar.activation(s_r[:], s_big[:], ACT.Copy, scale=neg_r[:])
-        nc.scalar.activation(pts[:], pt[:], ACT.Copy, scale=s_r[:])
-        y = tile("y", [P, I], F32)
-        y_sum = column("y_sum")
-        nc.vector.scalar_tensor_tensor(y[:], ta[:], neg_t[:], pc[:], ALU.add, ALU.mult, accum_out=y_sum[:])
-        beta = column("beta")
-        nc.vector.tensor_scalar(beta[:], s_big[:], neg_t[:], y_sum[:], ALU.mult, ALU.add)
-        rest = tile("rest", [P, I], F32)
-        nc.vector.scalar_tensor_tensor(rest[:], pn[:], beta[:], y[:], ALU.mult, ALU.add)
-        nc.vector.tensor_tensor(window[:].indirect(tok_list[:]), rest[:], pts[:], ALU.add)
+        neg_w = tile("neg_w", [P, I], F32)
+        nc.scalar.activation(neg_w[:], p[:], ACT.Copy, scale=neg_r[:])
+        w_c0 = tile("w_c0", [P, I], F32)
+        s_512 = column("s_512")
+        nc.vector.scalar_tensor_tensor(w_c0[:], c0[:], r_512[:], p[:], ALU.mult, ALU.mult, accum_out=s_512[:])
+        neg_s_r = column("neg_s_r")
+        nc.scalar.activation(neg_s_r[:], s_512[:], ACT.Copy, scale=neg_r[:])
+        term_ta = tile("term_ta", [P, I], F32)
+        nc.scalar.activation(term_ta[:], p_ta[:], ACT.Copy, scale=neg_s_r[:])
+        term_c0 = tile("term_c0", [P, I], F32)
+        term_c0_sum = column("term_c0_sum")
+        nc.vector.scalar_tensor_tensor(term_c0[:], ta[:], neg_t[:], w_c0[:], ALU.add, ALU.mult,
+                                       accum_out=term_c0_sum[:])
+        row_term = column("row_term")
+        nc.vector.tensor_scalar(row_term[:], s_512[:], neg_t[:], term_c0_sum[:], ALU.mult, ALU.add)
+        gs_but_ta = tile("gs_but_ta", [P, I], F32)
+        nc.vector.scalar_tensor_tensor(gs_but_ta[:], neg_w[:], row_term[:], term_c0[:], ALU.mult, ALU.add)
 
-        lo = 0
-        for n, width in enumerate(OUT_CHUNKS):
-            cols = slice(lo, lo + width)
-            res = tile("res%d" % n, [P, width], F32)
-            nc.vector.tensor_tensor(res[:], window[:, cols], base_sb[:, cols], ALU.add)
-            nc.sync.dma_start(out[:, cols], res[:])
-            lo += width
+        nc.vector.tensor_tensor(gf[:].indirect(tok_list[:]), gs_but_ta[:], term_ta[:], ALU.add)
+
+        for lo in range(0, T, OUT_CHUNK):
+            cols = slice(lo, lo + OUT_CHUNK)
+            result = tile("result%d" % lo, [P, OUT_CHUNK], F32)
+            nc.vector.tensor_tensor(result[:], gf[:, cols], base_sb[:, cols], ALU.add)
+            nc.sync.dma_start(out[:, cols], result[:])

from contextlib import ExitStack

import concourse.mybir as mybir

D, T, I, Q, G, U = 512, 2048, 512, 128, 64, 256
FLOPS = 2 * D * Q * (3 * I + G)

F32 = mybir.dt.float32
BF16 = mybir.dt.bfloat16
I32 = mybir.dt.int32
U32 = mybir.dt.uint32
U16 = mybir.dt.uint16
U8 = mybir.dt.uint8
FP8X4 = mybir.dt.float8_e4m3fn_x4
ALU = mybir.AluOpType
ACT = mybir.ActivationFunctionType

P = 128
PACK = 4
QUADRANT = 32
SCALE_ROWS = 4
LIST_GROUP = 16
PAGE = I // G
GS_SCALE = 512.0
V_SCALE_ROW0 = 4
OUT_CHUNK = 512


def tile_attend_hvpagetablegate_s_kernel(tc, query, pquery, keys_words, keys_scales, pgsum, reserve, gout,
                                          vals_words, vals_scales, dquery, base, offs2, offs, out):
    nc = tc.nc
    with ExitStack() as ctx:
        sb = ctx.enter_context(tc.tile_pool(name="sb", bufs=1))
        ps = ctx.enter_context(tc.psum_pool(name="ps", bufs=1))

        def tile(name, shape, dtype, reuse=None):
            return sb.tile(shape, dtype, name=name, tag=reuse or name, align_bytes=64)

        def column(name, reuse=None):
            return tile(name, [P, 1], F32, reuse)

        tok_list = tile("tok_list", [P, I // LIST_GROUP], U16)
        page_list = tile("page_list", [P, G // LIST_GROUP], U16)
        k_words = tile("k_words", [P, T], U32)
        v_words = tile("v_words", [P, T], U32)
        k_bytes = tile("k_bytes", [P, T], U8)
        v_bytes = tile("v_bytes", [P, T], U8)
        gf = tile("gf", [P, T], F32)
        base_sb = tile("base_sb", [P, T], F32)
        pg_raw = tile("pg_raw", [P, PACK, U], F32)
        reserve_sb = column("reserve_sb")

        nc.gpsimd.memset(k_bytes[:].bitcast(I32), 0)
        nc.gpsimd.memset(v_bytes[:].bitcast(I32), 0)
        nc.gpsimd.memset(gf[:], 0.0)

        def load_scale_bytes(dst, src, row0):
            for quad in range(P // QUADRANT):
                lo = QUADRANT * quad + row0
                rows = src[0, SCALE_ROWS * quad:SCALE_ROWS * (quad + 1), :]
                nc.sync.dma_start(dst[lo:lo + SCALE_ROWS, :].bitcast(I32), rows.bitcast(I32))

        def load_words(dst, src):
            nc.sync.dma_start(dst[:].bitcast(I32), src[0].rearrange("p n t -> p (n t)").bitcast(I32))

        def load_rows(name, src):
            raw = tile(name, [P, PACK, Q], F32)
            nc.sync.dma_start(raw[:], src.rearrange("(p t) w -> p t w", t=PACK))
            return raw

        nc.sync.dma_start(page_list[:], offs2)
        nc.sync.dma_start(tok_list[:], offs)
        nc.sync.dma_start(reserve_sb[:], reserve)
        nc.sync.dma_start(pg_raw[:], pgsum.rearrange("(p t) w -> p t w", t=PACK))
        pq_raw = load_rows("pq_raw", pquery)
        q_raw = load_rows("q_raw", query)
        load_scale_bytes(k_bytes, keys_scales, 0)
        load_words(k_words, keys_words)
        load_scale_bytes(v_bytes, vals_scales, V_SCALE_ROW0)
        dq_raw = load_rows("dq_raw", dquery)
        load_words(v_words, vals_words)
        go_raw = load_rows("go_raw", gout)
        nc.sync.dma_start(base_sb[:], base)

        def interleave(name, raw):
            grouped = tile(name, [P, Q, PACK], BF16)
            nc.scalar.copy(grouped[:], raw[:].rearrange("p t w -> p w t"))
            return grouped

        def quantize(name, grouped, width):
            codes = tile(name + "_codes", [P, width], U32)
            scales = tile(name + "_scales", [P, width], U8)
            nc.vector.quantize_mx(out=codes[:].bitcast(FP8X4), scales=scales[:],
                                  in_=grouped[:].rearrange("p w t -> p (w t)"))
            return codes, scales[:]

        def gather(name, pool_tile, dtype):
            picked = tile(name, [P, I], dtype)
            nc.vector.tensor_copy(picked[:], pool_tile[:].indirect(tok_list[:]))
            return picked

        def product(name, rows, columns, width):
            acc = ps.tile([P, width], F32, name=name)
            nc.tensor.matmul_mx(out=acc[:], lhsT=rows[0][:].bitcast(FP8X4), lhsT_scale=rows[1],
                                rhs=columns[0][:].bitcast(FP8X4), rhs_scale=columns[1], start=True, stop=True)
            return acc

        pg_bf = tile("pg_bf", [P, G, PACK], BF16)
        for t in range(PACK):
            nc.vector.tensor_copy(pg_bf[:, :, t], pg_raw[:, t, :].indirect(page_list[:]))
        reserve_512 = column("reserve_512")
        nc.scalar.mul(reserve_512[:], reserve_sb[:], 1.0 / GS_SCALE)
        pq_bf = interleave("pq_bf", pq_raw)
        q_bf = interleave("q_bf", q_raw)
        pg_mx = quantize("pg", pg_bf, G)
        k_bytes_listed = gather("k_bytes_listed", k_bytes, U8)
        pq_mx = quantize("pq", pq_bf, Q)
        h0 = product("h0", pq_mx, pg_mx, G)
        gate = tile("gate", [P, G, 1], F32)
        nc.scalar.activation(gate[:].rearrange("p g o -> p (g o)"), h0[:], ACT.Sigmoid)

        dq_bf = interleave("dq_bf", dq_raw)
        k_words_listed = gather("k_words_listed", k_words, U32)
        keys_mx = (k_words_listed, k_bytes_listed[:])
        q_mx = quantize("q", q_bf, Q)
        a = product("a", q_mx, keys_mx, I)
        v_bytes_listed = gather("v_bytes_listed", v_bytes, U8)
        dq_mx = quantize("dq", dq_bf, Q)
        ta = product("ta", dq_mx, keys_mx, I)

        neg_a = tile("neg_a", [P, I], F32, reuse="v_bytes")
        neg_m = column("neg_m")
        nc.vector.tensor_scalar(neg_a[:], a[:], -1.0, 0.0, ALU.mult, ALU.min, accum_out=neg_m[:])
        exp_a = tile("exp_a", [P, I], F32, reuse="dq_raw")
        nc.scalar.activation(exp_a[:], neg_a[:], ACT.Exp, bias=neg_m[:], scale=-1.0)
        exp_neg_m = column("exp_neg_m")
        nc.scalar.activation(exp_neg_m[:], neg_m[:], ACT.Exp)
        reserve_shifted = column("reserve_shifted")
        nc.scalar.activation(reserve_shifted[:], exp_neg_m[:], ACT.Copy, scale=reserve_512[:])
        go_bf = interleave("go_bf", go_raw)

        v_words_listed = gather("v_words_listed", v_words, U32)
        go_mx = quantize("go", go_bf, Q)
        c0 = product("c0", go_mx, (v_words_listed, v_bytes_listed[V_SCALE_ROW0:P, :]), I)

        p = tile("p", [P, I], F32, reuse="v_words")
        p_sum = column("p_sum")
        nc.vector.scalar_tensor_tensor(p[:].rearrange("p (g j) -> p g j", j=PAGE),
                                       exp_a[:].rearrange("p (g j) -> p g j", j=PAGE), 1.0,
                                       gate[:].to_broadcast([P, G, PAGE]), ALU.mult, ALU.mult, accum_out=p_sum[:])
        z_512 = column("z_512")
        nc.scalar.activation(z_512[:], p_sum[:], ACT.Identity, bias=reserve_shifted[:], scale=1.0 / GS_SCALE)
        r_512 = column("r_512", reuse="go_bf")
        nc.vector.reciprocal(r_512[:], z_512[:])
        neg_r = column("neg_r")
        nc.scalar.mul(neg_r[:], r_512[:], -1.0 / GS_SCALE)

        p_ta = tile("p_ta", [P, I], F32, reuse="z_512")
        tz = column("tz")
        nc.vector.scalar_tensor_tensor(p_ta[:], ta[:], 1.0, p[:], ALU.mult, ALU.mult, accum_out=tz[:])
        neg_t = column("neg_t")
        nc.scalar.activation(neg_t[:], tz[:], ACT.Copy, scale=neg_r[:])
        neg_w = tile("neg_w", [P, I], F32)
        nc.scalar.activation(neg_w[:], p[:], ACT.Copy, scale=neg_r[:])
        w_c0 = tile("w_c0", [P, I], F32)
        s_512 = column("s_512")
        nc.vector.scalar_tensor_tensor(w_c0[:], c0[:], r_512[:], p[:], ALU.mult, ALU.mult, accum_out=s_512[:])
        neg_s_r = column("neg_s_r")
        nc.scalar.activation(neg_s_r[:], s_512[:], ACT.Copy, scale=neg_r[:])
        term_ta = tile("term_ta", [P, I], F32)
        nc.scalar.activation(term_ta[:], p_ta[:], ACT.Copy, scale=neg_s_r[:])
        term_c0 = tile("term_c0", [P, I], F32)
        term_c0_sum = column("term_c0_sum")
        nc.vector.scalar_tensor_tensor(term_c0[:], ta[:], neg_t[:], w_c0[:], ALU.add, ALU.mult,
                                       accum_out=term_c0_sum[:])
        row_term = column("row_term")
        nc.vector.tensor_scalar(row_term[:], s_512[:], neg_t[:], term_c0_sum[:], ALU.mult, ALU.add)
        gs_but_ta = tile("gs_but_ta", [P, I], F32)
        nc.vector.scalar_tensor_tensor(gs_but_ta[:], neg_w[:], row_term[:], term_c0[:], ALU.mult, ALU.add)

        nc.vector.tensor_tensor(gf[:].indirect(tok_list[:]), gs_but_ta[:], term_ta[:], ALU.add)

        for lo in range(0, T, OUT_CHUNK):
            cols = slice(lo, lo + OUT_CHUNK)
            result = tile("result%d" % lo, [P, OUT_CHUNK], F32)
            nc.vector.tensor_tensor(result[:], gf[:, cols], base_sb[:, cols], ALU.add)
            nc.sync.dma_start(out[:, cols], result[:])
